import numpy as np, ml_dtypes
CORES = [40,64,80,88,96,104,120,144]
N = 8
import mx_ref
BF = ml_dtypes.bfloat16
def tile(rs):
    return np.stack(rs, axis=2).reshape(128, -1).astype(BF)
def pick(q, e):
    c = np.concatenate([q[0].reshape(128, -1, 4), np.zeros((128, 1, 4), np.uint8)], axis=1); s = np.concatenate([q[1], np.ones((16, 1), np.uint8)], axis=1)
    return (np.ascontiguousarray(c[:, e].reshape(128, -1)), np.ascontiguousarray(s[:, e]))
def join(*qs):
    return (np.concatenate([q[0] for q in qs], axis=1), np.concatenate([q[1] for q in qs], axis=1))
def put(q, e, v):
    c, s = q[0].reshape(128, -1, 4).copy(), q[1].copy(); c[:, e] = v[0].reshape(128, -1, 4); s[:, e] = v[1]
    return (c.reshape(128, -1), s)
def pk(c, s):
    return (np.ascontiguousarray(c), mx_ref.live(s))
def emit(q):
    return q[0], q[1]
def packed(v, rng):
    q = [mx_ref.quantize(np.ascontiguousarray(v[r])) for r in range(N)]
    return np.stack([a for a, b in q]), np.stack([mx_ref.plane(b, rng) for a, b in q])
def values_of_codes():
    e, c = np.zeros((128, 128, 4), np.float32), np.zeros((128, 2, 4), np.uint8)
    e[np.arange(128), np.arange(128), 0] = 1
    c[:127, :, 0] = np.arange(256).reshape(2, 128).T[:127]
    return mx_ref.matmul(mx_ref.quantize(e.reshape(128, 512).astype(BF)), (c.reshape(128, 8), np.full((16, 2), 127, np.uint8))).T.reshape(-1).astype(np.float64)
CODE_VALUE, SCALE_VALUE = values_of_codes(), 2.0 ** (np.arange(256) - 127.0)
def decode(q):
    return (CODE_VALUE[q[0]].reshape(16, 8, -1, 4) * SCALE_VALUE[q[1]][:, None, :, None] + 0.0).reshape(128, -1).astype(np.float32)
def f(rng, *shape):
    return mx_ref.flush((rng.standard_normal(shape, dtype=np.float32) * np.exp2(rng.integers(-2, 3, shape[:-1] + (1,)))).astype(BF))
def wide(rng, *shape, cols=0):
    v = rng.standard_normal(shape, dtype=np.float32) * np.exp2(rng.integers(-12, 13, shape)).astype(np.float32)
    if cols: v *= np.repeat(np.exp2(rng.integers(-cols, cols + 1, shape[:-2] + (1, shape[-1] // 4))) * (rng.random(shape[:-2] + (1, shape[-1] // 4)) > 0.0625), 4, axis=-1).astype(np.float32)
    return mx_ref.flush(v.astype(BF))
C, XOR = 256, [1, 2, 4]
def big(v):
    v = v.astype(np.float32)
    v[np.abs(v) < np.float32(2.0 ** -16)] = 0
    return v.astype(BF)
def numbers_of(rng):
    return {"x": big(f(rng, N, 128, 4 * C)), "u": np.array(f(rng, N, 128, 512)), "v": np.array(f(rng, N, 128, 512))}
def layers(rng):
    return big(f(rng, N, 128, 2048)).astype(np.float32).reshape(N, 8, 16, 4, 8, 16, 4)
def weights(rng, w):
    c, s = packed(np.ascontiguousarray(w).reshape(N, 128, 2048).astype(BF), rng)
    return {"wc": c, "ws": s}
def label(rng, d, e, k):
    x, u = d["x"].reshape(N, 8, 16, C, 4), d["u"].reshape(N, 128, 128, 4)
    d["u"].reshape(N, 128, 8, 16, 4)[:, :, :, :8] = 0
    for r in range(N):
        for g in range(8):
            o, a = rng.permutation(8), np.zeros((8, C), np.float32)
            a[o] = e[r, g]
            x[r, g, :2] = a.reshape(2, 4, C).transpose(0, 2, 1).astype(BF)
            for i in range(8): u[r, 16 * g + o[i] // 4, 16 * g + i, o[i] % 4] = float(k[r])
def setup_inputs(rng):
    return {**numbers_of(rng), **weights(rng, layers(rng))}
def setup_inputs_ties(rng):
    d = numbers_of(rng)
    o = rng.permutation(N)
    h = rng.permutation(8)[:4]
    e = rng.integers(0, 3, (N, 8, 8, C))
    e[o[2]] = 1
    e[o[3], h] = 0
    k = np.ones(N)
    k[o[0]], k[o[1]] = 0, -1
    label(rng, d, e, k)
    z = (N, 8, 8, C, 4)
    a = (1.125 + 0.25 * rng.integers(0, 4, z)) * np.exp2(rng.integers(-2, 5, z))
    a[:, :, 0, :, 0] = 1.96875 * 2.0 ** 12
    a = a * rng.choice([-1.0, 1.0], z)
    a[o[3], h, 1:3] = (1.375 + 0.25 * rng.integers(0, 2, (4, 2, C, 4))) * np.exp2(rng.integers(-2, 5, (4, 1, C, 1)))
    d["x"].reshape(N, 8, 16, C, 4)[:, :, 8:] = a.astype(np.float32).astype(BF)
    u = d["u"].reshape(N, 128, 128, 4)
    for g in h:
        for i in range(8): u[o[3], 16 * g + 9 + i // 4, 16 * g + i, i % 4] = 1.0
    w = layers(rng)
    w[:, :, 8] = 0
    w[:, :, :, :, :, [0, 1, 8]] = 0
    w[:, :, :, :, :, 9:] *= np.float32(0.125)
    return {**d, **weights(rng, w)}
def setup_inputs_near(rng):
    d = numbers_of(rng)
    x = d["x"].astype(np.float32).reshape(N, 8, 16, C, 4)
    x[:, :, :2] = 0
    x[:, :, 2:8] *= np.float32(0.125)
    x[:, :, 8:] = 0
    x[:, :, 0, :, 0] = rng.choice([-1.0, 1.0], (N, 8, C))
    x[:, :, 1, :, 0] = 2.0 ** -10
    x[:, :, 8:, :, 0] = rng.integers(0, 8, (N, 8, 8, C)) * 2.0 ** -23
    x[:, :, 8:12, :, 1] = 2.0 ** -30
    x[:, :, 12:, :, 1] = rng.choice([1.0, 1.125], (N, 8, 4, C)) * 2.0 ** -30
    u = d["u"].reshape(N, 128, 128, 4)
    d["u"].reshape(N, 128, 8, 16, 4)[:, :, :, :8] = 0
    o = rng.permutation(N) % 4
    for r in range(N):
        for g in rng.permutation(8)[:4]: x[r, g, 8 + rng.integers(8), rng.integers(C), 0] = 2.0 ** 14
        for h in range(0, 128, 16):
            far = int(rng.integers(8))
            for i in range(8):
                k = 1.0 if o[r] == 0 else 2.0 ** -30
                if o[r] < 2: u[r, h:h + 2, h + i, 0] = k
                if o[r] == 2 and i == far: u[r, h + 1, h + i, 0] = -1.0
                elif o[r] < 3: u[r, h + 8 + i, h + i, 0] = k
                else: u[r, h + 8 + i, h + i, 1] = k * 1.25 if i < 4 else k * 1.125
    w = layers(rng)
    for i in (0, 1, 8, 9, 10, 11, 12, 13, 14, 15):
        w[:, :, i] = 0
        w[:, :, :, :, :, i] = 0
    return {"x": x.reshape(N, 128, 4 * C).astype(BF), "u": d["u"], "v": d["v"], **weights(rng, w)}
def setup_inputs_huge(rng):
    d = numbers_of(rng)
    o = rng.permutation(N)
    a = rng.permuted(np.tile(np.repeat([2.0 ** 29, 2.0 ** 30], 256), (N, 64, 1)), axis=2).reshape(N, 8, 8, 512)
    for r in range(N):
        if o[r] < N // 2: a[r] *= (rng.permutation(8) % 2 * 2.0 - 1.0)[:, None, None]
        else:
            for g in range(8): a[r, g] *= (rng.permutation(8) % 2 * 2.0 - 1.0)[:, None]
    d["u"].reshape(N, 128, 8, 16, 4)[:, :, :, :8] = a.reshape(N, 8, 8, 128, 4).transpose(0, 3, 1, 2, 4).astype(np.float32).astype(BF)
    d["x"] = ((0.2 + 0.5 * rng.random((N, 128, 4 * C))) * 2.0 ** 29).astype(np.float32).astype(BF)
    return {**d, **weights(rng, layers(rng) * np.float32(2.0 ** -8))}
def setup_inputs_ends(rng):
    d = numbers_of(rng)
    o = rng.permutation(N) % 4
    z, k = np.where(o % 2 == 0, 2.0 ** 30, 2.0 ** -30), np.where(o < 2, 2.0 ** 30, 2.0 ** -30)
    s = rng.choice([-1.0, 1.0], (N, 128, 4 * C))
    s[o == 0] = 1.0
    d["x"] = (s * z[:, None, None]).astype(np.float32).astype(BF)
    for n in ("u", "v"): d[n] = (rng.choice([-1.0, 1.0], (N, 128, 512)) * k[:, None, None]).astype(np.float32).astype(BF)
    counts = [[3 * C + 1, 3 * C - 1, C, C - 1, 1, 0, 0, 0], [8 * C] + [0] * 7, [C] * 8, [C + 1, C - 1] + [C] * 6]
    e, i, low = np.zeros((N, 8, 8, C)), np.arange(8)[None, :, None], {}
    for r in range(N):
        if o[r] == 0:
            m, h, j = np.insert(rng.permutation(7) + 1, 2, 0), int(rng.integers(8)), int(rng.integers(C // 4))
            c = np.zeros((8, C), int)
            c[h] = m[0]
            c[np.ix_(np.delete(np.arange(8), h), np.delete(np.arange(C), j))] = rng.permutation(np.repeat(m, np.array(counts[0]) - np.array([C, 0, 7, 0, 0, 0, 0, 0]))).reshape(7, C - 1)
            c = c.reshape(8, 1, C)
            low[r] = (h, int(m[0]), j)
        else: c = rng.permutation(np.repeat(rng.permutation(8), counts[o[r]])).reshape(8, 1, C)
        equal = (rng.permutation(8) < 4)[:, None, None] & (rng.random((8, 8, C)) < 0.5)
        e[r] = np.where((i == c) | (i > c) & equal, z[r], -z[r])
    for r in low:
        e[r, low[r][0]] = z[r]
        e[r, :, :, low[r][2]] = z[r]
    label(rng, d, e, k)
    for r in low:
        h, m = low[r][:2]
        a = d["u"].reshape(N, 8, 16, 8, 16, 4)[r]
        a[:, 2:, :, :8] = -2.0 ** 30
        a[:, :, h, :8] = -2.0 ** 30
        a[h, 2, h, m, 0] = 0
    return {**d, **weights(rng, np.zeros((N, 128, 2048), np.float32))}
def setup_inputs_spread(rng):
    d = numbers_of(rng)
    d["x"] = big(wide(rng, N, 128, 4 * C, cols=6))
    return {**d, **weights(rng, layers(rng) * np.float32(0.25))}
def check_inputs(d):
    b = []
    for k in ("x", "u", "v"):
        a = np.abs(d[k].astype(np.float32))
        if not (np.isfinite(a).all() and ((a == 0) | (a >= 2.0 ** -30) & (a <= 2.0 ** 30)).all()): b.append("a value of " + k)
    none, least, most = [emit(mx_ref.quantize(np.full((128, 16), k, np.float32).astype(BF)))[1][0, 0] for k in (0.0, 2.0 ** -30, 2.0 ** 30)]
    m, t = float(np.max(np.abs(d["x"].astype(np.float32)))), 0.0
    for r in range(N):
        if ((d["wc"][r] == 0x7F) | (d["wc"][r] == 0xFF)).any(): b.append("wc: a code that is no number")
        s = mx_ref.live(d["ws"][r])
        if ((s != none) & ((s < least) | (s > most))).any(): b.append("ws: a scale out of range")
        w = np.abs(decode(pk(d["wc"][r], d["ws"][r]))).astype(np.float64).reshape(128, 512, 4)
        t = max(t, float(np.max(np.sum(w, axis=(0, 2)))))
    if not (t == 0 or m * (1 + t * 0.015625) ** 3 <= 2.0 ** 29): b.append("m * (1 + s * 0.015625)**3 is beyond 2**29, and s isn't 0")
    return b
def sources(c):
    e, over = np.full((8, C), -1), []
    for k in range(8):
        w = np.flatnonzero(c == k)
        e[k, :min(len(w), C)] = w[:C]
        over.append(w[C:])
    e[e < 0] = np.sort(np.concatenate(over))
    return e
def reference(x, u, v, wc, ws):
    qu = [mx_ref.quantize(u[r]) for r in range(N)]
    lay = [pk(wc[r], ws[r]) for r in range(N)]
    now = [x[r] for r in range(N)]
    y, om = np.zeros((N, 128, C), np.float32), np.zeros((N, 8, C), np.float32)
    oc, osc = np.zeros((N, 128, 4 * C), np.uint8), np.zeros((N, 16, C), np.uint8)
    for a in XOR:
        kept, sent = [], []
        for r in range(N):
            q = mx_ref.quantize(now[r])
            s = mx_ref.matmul(qu[r], q).reshape(8, 16, C)[:, :8] + np.float32(0.0)
            e = sources(np.argmax(s, axis=1).T.reshape(-1))
            t = decode(q).reshape(8, 16, C, 4).transpose(0, 2, 1, 3)
            made = t[e % 8, e // 8].transpose(0, 2, 1, 3).reshape(128, 4 * C).astype(BF)
            kept.append(made[:, :2 * C])
            sent.append(mx_ref.quantize(np.ascontiguousarray(made[:, 2 * C:])))
            om[r] = e
        for r in range(N):
            z = np.concatenate([kept[r], decode(sent[r ^ a]).astype(BF)], axis=1)
            q = mx_ref.quantize(z)
            now[r] = tile([mx_ref.matmul(pick(lay[r], np.arange(128 * b, 128 * b + 128)), q) * np.float32(0.015625) + z[:, b::4].astype(np.float32) for b in range(4)])
    for r in range(N):
        q = mx_ref.quantize(now[r])
        y[r] = mx_ref.matmul(mx_ref.quantize(v[r]), q)
        oc[r], osc[r] = emit(q)
    return {"y": y, "om": om, "oc": oc, "osc": osc}

from concourse.bass import DstId, RemoteDMATransfer
from concourse.mybir import dt, AluOpType as A, ActivationFunctionType as F

XOR = [1, 2, 4]
NREL = 4
PC = 128 // NREL
F8 = "float8_e4m3fn_x4"
BIG = 2.0 ** 90
M16, M256 = 1.5 * 2.0 ** 27, 1.5 * 2.0 ** 31

KN = {"tot": 0, "aa": 1, "ab": 2, "rc": 3, "x15": 4, "tri": 5, "s": 6, "w": 7, "z0": 8, "z1": 9, "z2": 10, "z3": 11,
      "o0": 12, "o1": 13, "o2": 14, "o3": 15, "n0": 16, "n1": 17, "n2": 18, "n3": 19}

SCRATCH = {
    "ub": ("sbuf", [128, 512], "bfloat16"), "vb": ("sbuf", [128, 512], "bfloat16"), "x0": ("sbuf", [128, 1024], "bfloat16"),
    "qu": ("sbuf", [128, 128], F8), "su": ("sbuf", [128, 128], "uint8"),
    "qu2": ("sbuf", [128, 128], F8), "su2": ("sbuf", [128, 128], "uint8"),
    "qv": ("sbuf", [128, 128], F8), "sv": ("sbuf", [128, 128], "uint8"),
    "qw": ("sbuf", [128, 512], F8), "sw": ("sbuf", [128, 512], "uint8"),
    "qx": ("sbuf", [128, 256], F8), "sx": ("sbuf", [128, 256], "uint8"),
    "eq": ("sbuf", [128, 4096], F8), "es": ("sbuf", [128, 4096], "uint8"),
    "kq": ("sbuf", [128, 2560], F8), "kqs": ("sbuf", [128, 2560], "uint8"),
    "kt0": ("sbuf", [128, 2048], "bfloat16"), "kt1": ("sbuf", [128, 2048], "bfloat16"),
    "ks": ("sbuf", [128, 10240], "bfloat16"),
    "mc": ("sbuf", [128, 128], "bfloat16"), "mx": ("sbuf", [128, 128], "bfloat16"), "mt": ("sbuf", [128, 128], "bfloat16"),
    "mr": ("sbuf", [128, 256], "bfloat16"), "i16": ("sbuf", [128, 16], "bfloat16"),
    "pc": ("sbuf", [128, 16], "int32"), "cf": ("sbuf", [128, 16], "float32"), "cm": ("sbuf", [128, 16], "float32"),
    "zm": ("sbuf", [128, 16], "float32"), "kb": ("sbuf", [128, 16], "float32"), "uo": ("sbuf", [128, 8], "uint16"),
    "gm": ("sbuf", [128, 128], "bfloat16"), "sg": ("sbuf", [128, 128], "bfloat16"), "hm": ("sbuf", [128, 128], "bfloat16"),
    "h1": ("sbuf", [128, 128], "bfloat16"), "i64": ("sbuf", [128, 128], "bfloat16"), "dx": ("sbuf", [128, 128], "bfloat16"),
    "nk": ("sbuf", [128, 128], "bfloat16"), "mm": ("sbuf", [128, 512], "bfloat16"),
    "rst": ("sbuf", [128, 256], "float32"), "zz": ("sbuf", [128, 64], "float32"),
    "st": ("sbuf", [128, 256], "float32"), "rm": ("sbuf", [128, 256], "float32"), "fb": ("sbuf", [128, 256], "bfloat16"),
    "ft": ("sbuf", [128, 512], "bfloat16"), "qf": ("sbuf", [128, 128], F8), "sf": ("sbuf", [128, 128], "uint8"),
    "pw": ("sbuf", [128, 128], "float32"), "tt": ("sbuf", [128, 256], "float32"),
    "vv": ("sbuf", [128, 130], "float32"), "r1": ("sbuf", [128, 130], "float32"), "dg": ("sbuf", [128, 1024], "bfloat16"),
    "qd": ("sbuf", [128, 256], F8), "sd": ("sbuf", [128, 256], "uint8"), "xi": ("sbuf", [128, 4], "float32"),
    "ac": ("sbuf", [128, 16], "float32"), "jk": ("sbuf", [128, 2048], "bfloat16"),
    "win": ("sbuf", [128, 8192], "bfloat16"), "hk": ("sbuf", [128, 512], "bfloat16"), "hc": ("sbuf", [128, 512], "bfloat16"),
    "z64": ("sbuf", [128, 512], "bfloat16"), "r64": ("sbuf", [128, 512], "float32"), "xt": ("sbuf", [128, 1024], "bfloat16"),
    "qz": ("sbuf", [128, 128], F8), "sz": ("sbuf", [128, 128], "uint8"),
    "yt": ("sbuf", [128, 256], "float32"), "omf": ("sbuf", [128, 256], "float32"),
}
for _h in range(2):
    SCRATCH.update({"li%d" % _h: ("sbuf", [128, 8], "uint16"), "wi%d" % _h: ("sbuf", [128, 8], "int32"),
                    "wd%d" % _h: ("sbuf", [128, 16], "int32"), "s2%d" % _h: ("sbuf", [128, 1024], "bfloat16"),
                    "q2%d" % _h: ("sbuf", [128, 256], F8), "c2%d" % _h: ("sbuf", [128, 256], "uint8"),
                    "lf%d" % _h: ("sbuf", [128, 32], "uint16")})
for _t in range(3):
    SCRATCH.update({"qy%d" % _t: ("sbuf", [128, 128], F8), "sy%d" % _t: ("sbuf", [128, 128], "uint8"),
                    "lq%d" % _t: ("sbuf", [128, 128], F8), "ls%d" % _t: ("sbuf", [128, 128], "uint8"),
                    "rq%d" % _t: ("sbuf", [128, PC], F8), "rs%d" % _t: ("sbuf", [128, 128], "uint8")})
PSUM = ["w0", "w1", "w2", "w3", "p0", "p1", "p2", "p3"]
for _b in PSUM:
    SCRATCH[_b] = ("psum", [128, 512], "float32")
SEMAPHORES = ["qg", "qv", "qs", "qp", "dx", "dxb", "du", "dv", "dwc", "dws", "dst", "loc"] + \
    ["%s%d" % (n, t) for n in ("arr", "in") for t in range(3)]


def relays(topo, core, partner):
    return [c for c in topo.cores_of(core) if c != core and topo.may_write(c, partner)][:NREL]


def bits(es):
    return sum(1 << e for e in es)


def hand_on(g, core, T, topo):
    mine = [c for c in topo.cores_of(core) if T.rank_of(c) is not None]
    if not mine:
        return
    home, sent = mine[0], 0
    for t in range(3):
        partner = T.cores[T.rank_of(home) ^ XOR[t]]
        rel = relays(topo, home, partner)
        if core not in rel:
            continue
        i = rel.index(core)
        rid, pid = topo.addr(partner, core)
        m, n = topo.mask(core, partner), len(topo.engines(core, partner))
        last = i == NREL - 1
        es = len(topo.engines(home, core))
        g.wait_ge(T.sem["in%d" % t], es // NREL + (es if last else 0))
        g.remote_dma(out_ap=T["lq%d" % t][:, PC * i:PC * i + PC].bitcast(dt.uint8), in_ap=T["rq%d" % t][:, 0:PC].bitcast(dt.uint8),
                     remote_sem=T.sem["arr%d" % t], local_sem=T.sem.loc, pid=pid, routing_id=rid, dma_engine_mask=m)
        sent += n
        if last:
            g.remote_dma(out_ap=T["ls%d" % t][:, 0:128], in_ap=T["rs%d" % t][:, 0:128],
                         remote_sem=T.sem["arr%d" % t], local_sem=T.sem.loc, pid=pid, routing_id=rid, dma_engine_mask=m)
            sent += n
    if sent:
        g.wait_ge(T.sem.loc, sent)


def machine(g, T):
    eng = {"g": g, "v": g.vector, "s": g.scalar, "p": g.tensor, "y": g.sync}
    own = {"g": "qg", "v": "qv", "s": "qs", "p": "qp"}
    clock = {q: {} for q in eng}
    count, regs = {}, {}

    def wait(q, tok):
        sem, n, clk = tok
        if clock[q].get(sem, 0) < n:
            eng[q].wait_ge(T.sem[sem], n)
            clock[q][sem] = n
            for k in clk:
                if clk[k] > clock[q].get(k, 0):
                    clock[q][k] = clk[k]

    def full(r):
        return r if len(r) == 4 else (r[0], r[1], r[2], 1)

    def meet(lo, hi, st, r):
        return r[0] < hi and lo < r[1] and not (st == r[5] and (lo - r[0]) % st)

    def inside(r, lo, hi, st):
        return lo <= r[0] and r[1] <= hi and (st == 1 or (st == r[5] and (lo - r[0]) % st == 0))

    def order(q, reads, writes):
        toks = []
        for n, lo, hi, st in map(full, reads):
            toks += [r[4] for r in regs.get(n, []) if (r[2] or (n in PSUM and r[3] != q)) and meet(lo, hi, st, r)]
        for n, lo, hi, st in map(full, writes):
            toks += [r[4] for r in regs.get(n, []) if (r[3] != q or q != "p") and meet(lo, hi, st, r)]
        best = {}
        for tok in toks:
            if tok[0] not in best or best[tok[0]][1] < tok[1]:
                best[tok[0]] = tok
        for tok in sorted(best.values(), key=lambda k: -len(k[2])):
            wait(q, tok)

    def note(q, tok, reads, writes):
        for n, lo, hi, st in map(full, reads):
            regs[n] = [r for r in regs.get(n, []) if not (r[3] == q and not r[2] and inside(r, lo, hi, st))]
            regs[n].append((lo, hi, False, q, tok, st))
        for n, lo, hi, st in map(full, writes):
            regs[n] = [r for r in regs.get(n, []) if not inside(r, lo, hi, st)]
            regs[n].append((lo, hi, True, q, tok, st))

    def op(q, call, reads, writes):
        order(q, reads, writes)
        sem = own[q]
        count[sem] = count.get(sem, 0) + 1
        call(eng[q]).then_inc(T.sem[sem], 1)
        note(q, (sem, count[sem], dict(clock[q])), reads, writes)

    def dma(q, call, reads, writes, sem):
        order(q, reads, writes)
        count[sem] = count.get(sem, 0) + 16
        call(eng[q]).then_inc(T.sem[sem], 16)
        note(q + sem, (sem, count[sem], dict(clock[q])), reads, writes)

    def arrive(sem, n, writes):
        note("far", (sem, n, {}), [], writes)

    def finish(extra):
        for sem in count:
            wait("y", (sem, count[sem], {}))
        for sem, n in extra:
            wait("y", (sem, n, {}))

    return op, dma, arrive, finish, order


def rank_program(g, core, T, topo):
    rank = T.rank_of(core)
    if rank is None:
        hand_on(g, core, T, topo)
        return
    op, dma, arrive, finish, order = machine(g, T)

    def mm(out, k, ks, a, q, s, b, n, start=True, stop=True):
        op("p", lambda e: e.matmul_mx(T[out][:, 0:n], T[k][:, a:a + 128], T[ks][:, a:a + 128], T[q][:, b:b + n], T[s][:, b:b + n], start, stop),
           [(k, a, a + 128), (q, b, b + n)], [(out, 0, 512)])

    def kmm(out, name, q, s, b, n=128, start=True, stop=True):
        mm(out, "kq", "kqs", 128 * KN[name], q, s, b, n, start, stop)

    def quant(q, s, a, n, src, b):
        op("v", lambda e: e.quantize_mx(T[q][:, a:a + n], T[s][:, a:a + n], T[src][:, b:b + 4 * n]),
           [(src, b, b + 4 * n)], [(q, a, a + n)])

    def ts(out, in0, s1, s2, o0, o1, reads, writes):
        if o1 is None:
            op("v", lambda e: e.tensor_scalar(out, in0, s1, None, o0), reads, writes)
        else:
            op("v", lambda e: e.tensor_scalar(out, in0, s1, s2, o0, o1), reads, writes)

    def tt(out, a, b, o, reads, writes):
        op("v", lambda e: e.tensor_tensor(out, a, b, o), reads, writes)

    def copy(out, in_, reads, writes):
        op("v", lambda e: e.tensor_copy(out, in_), reads, writes)

    def fill(buf, a, b, val, step=1):
        op("v", lambda e: e.memset(T[buf][:, a:b:step], val), [], [(buf, a, b, step)])

    def act(out, in_, func, reads, writes, **kw):
        op("s", lambda e: e.activation(out, in_, func, **kw), reads, writes)

    def iota(buf, a, b, pattern, base, cmul):
        kw = {} if buf == "pc" else {"allow_small_or_imprecise_dtypes": True}
        op("g", lambda e: e.iota(T[buf][:, a:b], pattern, base, cmul, **kw), [], [(buf, a, b)])

    dma("y", lambda e: e.dma_start(T.ub[:, :], T.u[:, :]), [], [("ub", 0, 512)], "du")
    dma("s", lambda e: e.dma_start(T.x0[:, 0:512], T.x[:, 0:512]), [], [("x0", 0, 512)], "dx")
    dma("y", lambda e: e.dma_start(T.x0[:, 512:1024], T.x[:, 512:1024]), [], [("x0", 512, 1024)], "dxb")
    dma("y", lambda e: e.dma_start(T.qw[:, :].bitcast(dt.uint8), T.wc[:, :]), [], [("qw", 0, 512)], "dwc")
    dma("y", lambda e: e.dma_start(T.sw[:, :], T.ws[:, :]), [], [("sw", 0, 512)], "dws")
    dma("y", lambda e: e.dma_start(T.vb[:, :], T.v[:, :]), [], [("vb", 0, 512)], "dv")

    iota("pc", 0, 1, [[0, 1]], 0, 1)
    iota("mx", 0, 128, [[0, 8], [1, 16]], 0, 0)
    iota("mr", 0, 256, [[1, 256]], 0, 0)
    iota("mc", 0, 128, [[1, 8], [0, 16]], 0, 0)
    iota("i16", 0, 16, [[16, 16]], 0, 0)
    iota("mt", 0, 128, [[0, 8], [1, 4], [0, 4]], 0, 0)
    iota("kt1", 0, 2048, [[0, 2048]], 0, 0)
    fill("kt0", 0, 2048, 0.0)
    P = [("pc", 0, 1)]
    ts(T.pc[:, 1:2], T.pc[:, 0:1], 15, None, A.bitwise_and, None, P, [("pc", 1, 2)])
    ts(T.pc[:, 2:3], T.pc[:, 0:1], 4, None, A.arith_shift_right, None, P, [("pc", 2, 3)])
    ts(T.pc[:, 3:4], T.pc[:, 0:1], 3, None, A.bitwise_and, None, P, [("pc", 3, 4)])
    ts(T.pc[:, 4:5], T.pc[:, 0:1], 2, 3, A.arith_shift_right, A.bitwise_and, P, [("pc", 4, 5)])
    ts(T.pc[:, 5:6], T.pc[:, 0:1], 7, None, A.bitwise_and, None, P, [("pc", 5, 6)])
    copy(T.cf[:, 0:6], T.pc[:, 0:6], [("pc", 0, 6)], [("cf", 0, 6)])
    ts(T.cf[:, 6:7], T.cf[:, 1:2], 1.0, None, A.add, None, [("cf", 1, 2)], [("cf", 6, 7)])
    ts(T.cf[:, 7:8], T.cf[:, 2:3], 256.0, None, A.mult, None, [("cf", 2, 3)], [("cf", 7, 8)])
    ts(T.cf[:, 8:9], T.cf[:, 3:4], 2048.0, None, A.mult, None, [("cf", 3, 4)], [("cf", 8, 9)])
    CF = [("cf", 0, 9)]
    ts(T.gm[:, :], T.mx[:, :], T.cf[:, 1:2], None, A.is_equal, None, CF + [("mx", 0, 128)], [("gm", 0, 128)])
    ts(T.cm[:, 0:8], T.mr[:, 0:8], T.cf[:, 2:3], None, A.is_equal, None, CF + [("mr", 0, 256)], [("cm", 0, 8)])

    def e_tiles(gr):
        kt = "kt%d" % (gr % 2)
        for b in range(4):
            act(T[kt][:, 512 * b + b:512 * b + 512:4], T.gm[:, :], F.Identity, [("gm", 0, 128), ("cm", 0, 8)],
                [(kt, 512 * b + b, 512 * b + 512, 4)], scale=T.cm[:, gr:gr + 1])
        quant("eq", "es", 512 * gr, 512, kt, 0)

    def slot(name, t):
        a = 512 * KN[name]
        return T.ks[:, a + t:a + 512:4], [("ks", a + t, a + 512, 4)]

    e_tiles(0)
    ts(T.uo[:, 0:8], T.i16[:, 0:8], T.cf[:, 5:6], None, A.add, None, CF + [("i16", 0, 16)], [("uo", 0, 8)])
    ts(T.kb[:, :], T.i16[:, :], T.cf[:, 1:2], 0.5, A.add, A.add, CF + [("i16", 0, 16)], [("kb", 0, 16)])
    ts(T.zm[:, 0:4], T.mr[:, 0:4], T.cf[:, 4:5], None, A.is_equal, None, CF + [("mr", 0, 256)], [("zm", 0, 4)])
    ts(T.zm[:, 4:8], T.mr[:, 0:4], T.cf[:, 3:4], None, A.is_equal, None, CF + [("mr", 0, 256)], [("zm", 4, 8)])
    ts(T.hm[:, :], T.mc[:, :], T.cf[:, 1:2], None, A.is_equal, None, CF + [("mc", 0, 128)], [("hm", 0, 128)])
    ts(T.h1[:, :], T.mc[:, :], T.cf[:, 6:7], None, A.is_equal, None, CF + [("mc", 0, 128)], [("h1", 0, 128)])
    ts(T.dx[:, :], T.mx[:, :], T.cf[:, 2:3], None, A.subtract, None, CF + [("mx", 0, 128)], [("dx", 0, 128)])
    tt(T.nk[:, :], T.h1[:, :], T.hm[:, :], A.subtract, [("h1", 0, 128), ("hm", 0, 128)], [("nk", 0, 128)])
    e_tiles(1)
    NK = [("nk", 0, 128)]
    for t in range(4):
        o, w = slot("tot", t)
        act(o, T.nk[:, :], F.Identity, NK, w, scale=-1.0)
    for t in range(2):
        ts(T.mm[:, 128 * t:128 * t + 128], T.dx[:, :], 8.0 * t, None, A.is_lt, None, [("dx", 0, 128)], [("mm", 128 * t, 128 * t + 128)])
        fill("ks", 512 * KN["ab"] + t, 512 * KN["ab"] + 512, 0.0, 4)
    for t in range(2):
        o, w = slot("aa", t)
        tt(o, T.mm[:, 128 * t:128 * t + 128], T.nk[:, :], A.mult, NK + [("mm", 128 * t, 128 * t + 128)], w)
        o, w = slot("ab", t + 2)
        tt(o, T.mm[:, 128 * t:128 * t + 128], T.nk[:, :], A.mult, NK + [("mm", 128 * t, 128 * t + 128)], w)
        o, w = slot("aa", t + 2)
        act(o, T.nk[:, :], F.Identity, NK, w)
    quant("kq", "kqs", 0, 128 * 3, "ks", 0)

    quant("qu", "su", 0, 128, "ub", 0)
    copy(T.qu2[:, 0:128].bitcast(dt.uint32), T.qu[:, 0:128].bitcast(dt.uint32).indirect(T.uo[:, 0:8]), [("qu", 0, 128), ("uo", 0, 8)], [("qu2", 0, 128)])
    act(T.su2[:, 0:128], T.su[:, 0:128].indirect(T.uo[:, 0:8]), F.Copy, [("qu", 0, 128), ("uo", 0, 8)], [("su2", 0, 128)])
    fill("rst", 0, 256, BIG)
    fill("zz", 0, 64, 0.0)
    fill("fb", 248, 256, 0.0)
    fill("ft", 256, 512, 0.0)
    fill("rst", 0, 256, -BIG, 16)
    quant("qx", "sx", 0, 128, "x0", 0)
    quant("qx", "sx", 128, 128, "x0", 512)

    def more_constants():
        ts(T.sg[:, :], T.mc[:, :], T.cf[:, 2:3], None, A.is_equal, None, CF + [("mc", 0, 128)], [("sg", 0, 128)])
        ts(T.i64[:, :], T.mr[:, 0:128], T.cf[:, 0:1], 64.0, A.is_equal, A.mult, CF + [("mr", 0, 256)], [("i64", 0, 128)])
        ts(T.mm[:, 0:128], T.mc[:, :], T.cf[:, 2:3], None, A.is_gt, None, CF + [("mc", 0, 128)], [("mm", 0, 128)])
        ts(T.cm[:, 8:9], T.cf[:, 1:2], 0.0, None, A.is_equal, None, CF, [("cm", 8, 9)])
        ts(T.cm[:, 9:10], T.cf[:, 1:2], 15.0, None, A.is_equal, None, CF, [("cm", 9, 10)])
        ts(T.mm[:, 128:256], T.mt[:, :], T.cf[:, 3:4], 32.0, A.is_equal, A.mult, CF + [("mt", 0, 128)], [("mm", 128, 256)])
        for t in range(3):
            o, w = slot("rc", t)
            copy(o, T.gm[:, :], [("gm", 0, 128)], w)
            o, w = slot("x15", t)
            ts(o, T.mr[:, 0:128], 0.0, T.cm[:, 9:10], A.is_ge, A.mult, [("mr", 0, 256), ("cm", 9, 10)], w)
            o, w = slot("tri", t)
            ts(o, T.mm[:, 0:128], T.cm[:, 8:9], None, A.mult, None, [("mm", 0, 128), ("cm", 8, 9)], w)
        for n in ("rc", "x15", "tri"):
            fill("ks", 512 * KN[n] + 3, 512 * KN[n] + 512, 0.0, 4)
        fill("dg", 0, 1024, 0.0)
        quant("kq", "kqs", 128 * 3, 128 * 3, "ks", 512 * 3)
        quant("qd", "sd", 0, 256, "dg", 0)
        fill("vv", 128, 130, 0.0)

    def list_constants():
        for t in range(4):
            a = 256 + 128 * (t % 2)
            ts(T.mm[:, a:a + 128], T.mt[:, :], float(t), None, A.is_equal, None, [("mt", 0, 128)], [("mm", a, a + 128)])
            o, w = slot("s", t)
            tt(o, T.mm[:, a:a + 128], T.sg[:, :], A.mult, [("mm", a, a + 128), ("sg", 0, 128)], w)
        a = 512 * KN["w"]
        fill("ks", a, a + 512, 0.0)
        for h in range(2):
            fill("s2%d" % h, 0, 1024, 0.0)
        o, w = slot("w", 0)
        tt(o, T.mm[:, 128:256], T.sg[:, :], A.mult, [("mm", 128, 256), ("sg", 0, 128)], w)
        for h in range(2):
            quant("q2%d" % h, "c2%d" % h, 0, 256, "s2%d" % h, 0)
        quant("kq", "kqs", 128 * 6, 256, "ks", 512 * 6)

    def layer_constants():
        a = 512 * KN["z0"]
        fill("ks", a, a + 2048, 0.0)
        for b in range(4):
            o, w = slot("z%d" % b, b)
            copy(o, T.i64[:, :], [("i64", 0, 128)], w)
        quant("kq", "kqs", 128 * KN["z0"], 512, "ks", a)

    def om_constants():
        a = 512 * KN["o0"]
        fill("ks", a, a + 4096, 0.0)
        for t in range(4):
            o, w = slot("o%d" % t, t)
            copy(o, T.sg[:, :], [("sg", 0, 128)], w)
            o, w = slot("n%d" % t, 0)
            ts(o, T.sg[:, :], T.zm[:, 4 + t:5 + t], 32.0, A.mult, A.mult, [("sg", 0, 128), ("zm", 0, 8)], w)
        quant("kq", "kqs", 128 * KN["o0"], 512, "ks", a)
        quant("kq", "kqs", 128 * KN["n0"], 512, "ks", a + 2048)
        quant("qv", "sv", 0, 128, "vb", 0)

    def one_round(t):
        steps = [(gr, b) for gr in range(8) for b in range(4)]
        at = [0]

        def pump(n, who="s"):
            for gr, b in steps[at[0]:at[0] + n]:
                bank = "w%d" % (at[0] % 4)
                mm(bank, "eq", "es", 512 * gr + 128 * b, "qx", "sx", 0, 256)
                a = 2048 * b + gr
                o, i, w = T.win[:, a:2048 * b + 2048:8], T[bank][:, 0:256], [("win", a, 2048 * b + 2048, 8)]
                if who == "s":
                    act(o, i, F.Copy, [(bank, 0, 512)], w)
                else:
                    copy(o, i, [(bank, 0, 512)], w)
                at[0] += 1

        order("p", [("su2", 0, 128)], [])
        mm("p0", "qu2", "su2", 0, "qx", "sx", 0, 256)
        if t == 0:
            e_tiles(2)
        pump(8)
        op("v", lambda e: e.transpose(T.st[:, :], T.p0[:, 0:256]), [("p0", 0, 512)], [("st", 0, 256)])
        op("v", lambda e: e.tensor_tensor_scan(T.rm[:, :], T.rst[:, :], T.st[:, :], 0.0, A.min, A.max),
           [("rst", 0, 256), ("st", 0, 256)], [("rm", 0, 256)])
        tt(T.fb[:, 0:248], T.rm[:, 0:248], T.rm[:, 8:256], A.is_ge, [("rm", 0, 256)], [("fb", 0, 248)])
        op("v", lambda e: e.transpose(T.ft[:, 0:256], T.fb[:, :]), [("fb", 0, 256)], [("ft", 0, 256)])
        quant("qf", "sf", 0, 128, "ft", 0)
        kmm("p1", "tot", "qf", "sf", 0)
        kmm("p2", "aa", "qf", "sf", 0)
        kmm("p3", "ab", "qf", "sf", 0)
        if t == 0:
            for gr in (3, 4):
                e_tiles(gr)
            more_constants()
        pump(8)
        op("v", lambda e: e.tensor_tensor_scan(T.pw[:, 0:64], T.zz[:, :], T.p1[:, 0:64], 0.0, A.add, A.add),
           [("zz", 0, 64), ("p1", 0, 512)], [("pw", 0, 64)])
        tt(T.tt[:, 0:64], T.p2[:, 0:64], T.pw[:, 0:64], A.add, [("p2", 0, 512), ("pw", 0, 64)], [("tt", 0, 64)])
        tt(T.tt[:, 128:192], T.p3[:, 0:64], T.pw[:, 0:64], A.add, [("p3", 0, 512), ("pw", 0, 64)], [("tt", 128, 192)])
        ts(T.vv[:, 128:129], T.pw[:, 63:64], 256.0, None, A.min, None, [("pw", 0, 64)], [("vv", 128, 129)])
        ts(T.vv[:, 0:64], T.tt[:, 0:64], -256.0, 0.0, A.add, A.max, [("tt", 0, 64)], [("vv", 0, 64)])
        ts(T.vv[:, 64:128], T.tt[:, 128:192], -256.0, 0.0, A.add, A.max, [("tt", 128, 192)], [("vv", 64, 128)])
        V = [("vv", 0, 130)]
        ts(T.r1[:, :], T.vv[:, :], M16, -M16, A.add, A.add, V, [("r1", 0, 130)])
        ts(T.dg[:, 2:520:4], T.vv[:, :], M256, -M256, A.add, A.add, V, [("dg", 2, 520, 4)])
        tt(T.dg[:, 0:520:4], T.vv[:, :], T.r1[:, :], A.subtract, V + [("r1", 0, 130)], [("dg", 0, 520, 4)])
        tt(T.dg[:, 1:520:4], T.r1[:, :], T.dg[:, 2:520:4], A.subtract, [("r1", 0, 130), ("dg", 2, 520, 4)], [("dg", 1, 520, 4)])
        quant("qd", "sd", 0, 130, "dg", 0)
        kmm("p0", "tri", "qd", "sd", 128)
        kmm("p1", "x15", "qd", "sd", 64)
        kmm("p2", "rc", "qd", "sd", 0)
        if t == 0:
            for gr in (5, 6, 7):
                e_tiles(gr)
            list_constants()
        pump(8)
        N = T.pw[:, 63:64]
        ts(T.xi[:, 0:1], T.p0[:, 0:1], N, T.cf[:, 7:8], A.add, A.subtract, CF + [("p0", 0, 512), ("pw", 0, 64)], [("xi", 0, 1)])
        XI = [("xi", 0, 1), ("pw", 0, 64)]
        ts(T.pw[:, 64:128], T.p1[:, 0:64], T.xi[:, 0:1], N, A.add, A.max, XI + [("p1", 0, 512)], [("pw", 64, 128)])
        ts(T.tt[:, 64:128], T.p2[:, 0:64], T.xi[:, 0:1], N, A.add, A.max, XI + [("p2", 0, 512)], [("tt", 64, 128)])
        ts(T.tt[:, 192:256], T.p2[:, 64:128], T.xi[:, 0:1], N, A.add, A.max, XI + [("p2", 0, 512)], [("tt", 192, 256)])

        def words(h):
            for k in range(8 * h, 8 * h + 8):
                act(T.jk[:, 128 * k:128 * k + 128], T.pw[:, 0:128], F.Sign, [("pw", 0, 128), ("kb", 0, 16)],
                    [("ac", k, k + 1), ("jk", 128 * k, 128 * k + 128)], bias=T.kb[:, k:k + 1], scale=-1.0, accum_out=T.ac[:, k:k + 1])

        def places(h, bank):
            li, wi, wd, s2, q2, c2, lf = ["%s%d" % (n, h) for n in ("li", "wi", "wd", "s2", "q2", "c2", "lf")]
            acc, R = T.ac[:, 8 * h:8 * h + 8], [("ac", 8 * h, 8 * h + 8)]
            ts(T[li][:, 0:8], acc, 0.5, 64.0, A.mult, A.add, R, [(li, 0, 8)])
            ts(T[wi][:, 0:8], acc, 0.5, 64.0, A.mult, A.add, R, [(wi, 0, 8)])
            for i in range(2):
                tt(T[s2][:, 128 * i:128 * i + 128], T.tt[:, 128 * i:128 * i + 128].indirect(T[li][:, 0:8]), T.mr[:, 128 * h:128 * h + 128],
                   A.is_le, [("tt", 128 * i, 128 * i + 128), (li, 0, 8), ("mr", 0, 256)], [(s2, 128 * i, 128 * i + 128)])
                ts(T[wd][:, 8 * i:8 * i + 8], T[wi][:, 0:8], (48, 15)[i], None, A.bitwise_and, None, [(wi, 0, 8)], [(wd, 8 * i, 8 * i + 8)])
            for z in range(4):
                ts(T[s2][:, 256 + 4 * z:512:16], T[wd][:, 0:16], T.zm[:, z:z + 1], None, A.mult, None, [(wd, 0, 16), ("zm", 0, 4)],
                   [(s2, 256 + 4 * z, 512, 16)])
            quant(q2, c2, 0, 128, s2, 0)
            for i in range(4):
                kmm(bank, "ssww"[i], q2, c2, 32 * i, 128, i == 0, i == 3)
            ts(T[lf][:, 0:32], T[bank][:, 0:32], T.cf[:, 8:9], None, A.add, None, CF + [(bank, 0, 512)], [(lf, 0, 32)])

        def gather(h, dst):
            lf = "lf%d" % h
            R = [("win", 0, 8192), (lf, 0, 32)]
            copy(T[dst][:, 0:256], T.win[:, 0:8192].indirect(T[lf][:, 0:16]), R, [(dst, 0, 256)])
            act(T[dst][:, 256:512], T.win[:, 0:8192].indirect(T[lf][:, 16:32]), F.Copy, R, [(dst, 256, 512)])

        def om_half(h):
            for i in range(4):
                bank = "w%d" % i
                for j in range(4):
                    kmm(bank, ("o%d" if j < 2 else "n%d") % i, "q2%d" % h, "c2%d" % h, 32 * j, 128, j == 0, j == 3)
                act(T.omf[:, 128 * h + i:128 * h + 128:4], T[bank][:, 0:32], F.Copy, [(bank, 0, 512)], [("omf", 128 * h + i, 128 * h + 128, 4)])

        words(1)
        pump(8, "v")
        words(0)
        places(1, "p3")
        gather(1, "hc")
        qy, sy = "qy%d" % t, "sy%d" % t
        quant(qy, sy, 0, 128, "hc", 0)
        partner = T.cores[rank ^ XOR[t]]
        rel = relays(topo, core, partner)
        order("g", [(qy, 0, 128)], [])
        moves = []
        for i, c in enumerate(rel):
            rid, pid = topo.addr(c, core)
            es = topo.engines(core, c)
            k = len(es) // NREL
            moves.append(RemoteDMATransfer(dst_ids=[DstId(rid=rid, pnc=pid)], dma_engine_mask=bits(es[k * i:k * i + k]),
                                           remote_sem=T.sem["in%d" % t], src=T[qy][:, PC * i:PC * i + PC].bitcast(dt.uint8),
                                           dst=T["rq%d" % t][:, 0:PC].bitcast(dt.uint8)))
        g.remote_dma_fused(moves, local_sem=T.sem.loc)
        c = rel[-1]
        rid, pid = topo.addr(c, core)
        g.remote_dma(out_ap=T["rs%d" % t][:, 0:128], in_ap=T[sy][:, 0:128], remote_sem=T.sem["in%d" % t], local_sem=T.sem.loc,
                     pid=pid, routing_id=rid, dma_engine_mask=topo.mask(core, c))
        places(0, "p0")
        gather(0, "hk")
        quant("qz", "sz", 0, 128, "hk", 0)
        act(T.z64[:, :], T.hk[:, :], F.Identity, [("hk", 0, 512)], [("z64", 0, 512)], scale=64.0)
        if t == 0:
            layer_constants()
            order("p", [("sw", 0, 512)], [])
        for b in range(4):
            mm("w%d" % b, "qw", "sw", 128 * b, "qz", "sz", 0, 128)
        for b in range(4):
            r = [("r64", 128 * b, 128 * b + 128)]
            tt(T.r64[:, 128 * b:128 * b + 128], T["w%d" % b][:, 0:128], T.z64[:, b:512:4], A.add, [("w%d" % b, 0, 512), ("z64", 0, 512)], r)
            act(T.xt[:, b:512:4], T.r64[:, 128 * b:128 * b + 128], F.Identity, r, [("xt", b, 512, 4)], scale=0.015625)
        quant("qx", "sx", 0, 128, "xt", 0)
        if t == 1:
            om_constants()
        if t == 2:
            om_half(1)
            om_half(0)
        lq, ls = "lq%d" % t, "ls%d" % t
        far = [len(topo.engines(c, core)) for c in relays(topo, partner, core)]
        arrive("arr%d" % t, sum(far) + far[-1], [(lq, 0, 128)])
        for b in range(4):
            bank = "p%d" % b
            mm(bank, "qw", "sw", 128 * b, lq, ls, 0, 128, True, False)
            kmm(bank, "z%d" % b, lq, ls, 0, 128, False, True)
            o, i, w = T.xt[:, 512 + b:1024:4], T[bank][:, 0:128], [("xt", 512 + b, 1024, 4)]
            if b % 2 == 0:
                act(o, i, F.Identity, [(bank, 0, 512)], w, scale=0.015625)
            else:
                ts(o, i, 0.015625, None, A.mult, None, [(bank, 0, 512)], w)
        quant("qx", "sx", 128, 128, "xt", 512)

    for t in range(3):
        one_round(t)

    mm("w0", "qv", "sv", 0, "qx", "sx", 0, 256)
    copy(T.yt[:, 0:256], T.w0[:, 0:256], [("w0", 0, 512)], [("yt", 0, 256)])
    dma("y", lambda e: e.dma_start(T.om[:, :], T.omf[0:128:16, :]), [("omf", 0, 256)], [], "dst")
    dma("y", lambda e: e.dma_start(T.oc[:, :], T.qx[:, 0:256].bitcast(dt.uint8)), [("qx", 0, 256)], [], "dst")
    for k in range(4):
        dma("s", lambda e: e.dma_start(T.osc[4 * k:4 * k + 4, :], T.sx[32 * k:32 * k + 4, 0:256]), [("qx", 0, 256)], [], "dst")
    dma("y", lambda e: e.dma_start(T.y[:, :], T.yt[:, :]), [("yt", 0, 256)], [], "dst")
    n = 0
    for t in range(3):
        rel = relays(topo, core, T.cores[rank ^ XOR[t]])
        n += sum(len(topo.engines(core, c)) // NREL for c in rel) + len(topo.engines(core, rel[-1]))
    finish([("loc", n)])
